import numpy as np
import ml_dtypes


def mxq(x, axis, fmt="e4m3"):
    dtype, down = {"e4m3": (ml_dtypes.float8_e4m3fn, 7), "e5m2": (ml_dtypes.float8_e5m2, 14)}[fmt]
    v = np.moveaxis(np.asarray(x, np.float32).astype(ml_dtypes.bfloat16).astype(np.float64), axis, -1)
    blocks = v.reshape(v.shape[:-1] + (-1, 32))
    amax = np.abs(blocks).max(-1, keepdims=True)
    byte = np.maximum(np.where(amax > 0, np.frexp(amax)[1] - 1 + 127, 0) - down, 1)
    scale = np.exp2(byte - 127.0)
    codes = (blocks / scale).astype(np.float32).astype(dtype).astype(np.float64)
    return np.moveaxis((codes * scale).reshape(v.shape), -1, axis)


WIDE = False


def mx_kscale(k):
    if not WIDE:
        return np.ones(k)
    levels = np.array([10, -10, 5, -5, 0])
    if k % 512:
        return np.exp2(np.random.permutation(np.resize(levels, k // 32))).repeat(32)
    a = np.empty((k // 512, 16))
    for p in range(k // 512):
        a[p, :8] = np.random.permutation(np.resize(levels, 8))
        for g in range(8):
            far = levels[np.abs(levels - a[p, g]) >= 10]
            a[p, g + 8] = far[np.random.randint(len(far))]
    return np.exp2(a.ravel()).repeat(32)


def f64(x):
    return np.asarray(x).astype(np.float64)


def striped(idx):
    return np.tile(idx.reshape(-1, 16).T, (8, 1)).astype(np.uint16)


def unstriped(offs):
    return offs[:16].T.reshape(-1).astype(np.int64)


def pack_weight(w):
    k, n = w.shape
    w = f64(np.asarray(w, np.float32).astype(ml_dtypes.bfloat16)).reshape(k // 32, 32, n)
    amax = np.abs(w).max(1)
    byte = np.clip(np.where(amax > 0, np.frexp(amax)[1] - 1 + 127 - 7, 1), 1, 254)
    scaled = (w * np.exp2(127.0 - byte)[:, None, :]).reshape(k, n).astype(np.float32)
    words = np.ascontiguousarray(scaled.reshape(k // 512, 128, 4, n).transpose(0, 1, 3, 2)).astype(ml_dtypes.float8_e4m3fn).view(np.uint8)
    return words, np.ascontiguousarray(byte.astype(np.uint8).reshape(k // 512, 16, n))


def unpack_weight(words, scales):
    g, p, n, _ = words.shape
    vals = np.ascontiguousarray(words).view(ml_dtypes.float8_e4m3fn).astype(np.float64) * np.repeat(np.exp2(scales.astype(np.float64) - 127.0), 8, axis=1)[..., None]
    return vals.transpose(0, 1, 3, 2).reshape(g * 512, n)


def planes(y):
    n, m = y.shape
    v = y.astype(np.float32).astype(ml_dtypes.bfloat16).astype(np.float64).reshape(n // 32, 32, m)
    top = np.abs(v).max(1)
    byte = np.clip(np.where(top > 0, np.frexp(top)[1] - 1 + 127 - 7, 1), 1, 254)
    codes = (v * np.exp2(127.0 - byte)[:, None, :]).reshape(n, m).astype(np.float32).astype(ml_dtypes.float8_e4m3fn).view(np.uint8)
    words = codes.reshape(n // 512, 128, 4, m).transpose(0, 1, 3, 2)
    return np.ascontiguousarray(words), np.ascontiguousarray(byte.astype(np.uint8).reshape(n // 512, 16, m))


def relu(v):
    return np.maximum(v, 0.0)


K, T, S, N = 512, 2048, 512, 512


def setup_inputs():
    n = np.random.standard_normal
    s = mx_kscale(K)[:, None]
    packed_xT = pack_weight(n((K, T)) * s)
    return {
        "x_words": packed_xT[0],
        "x_scales": packed_xT[1],
        "w1": (n((K, N)) / np.sqrt(K) / s).astype(np.float32),
        "w2": (n((K, N)) / np.sqrt(K) / s).astype(np.float32),
        "feat": (n((N, S))).astype(np.float32),
        "offs": striped(np.random.permutation(T)[:S]),
    }


def reference(x_words, x_scales, w1, w2, feat, offs):
    xq = unpack_weight(x_words, x_scales)[:, unstriped(offs)]
    g = mxq(f64(w1), 0, "e4m3").T @ xq
    h = mxq(f64(w2), 0, "e4m3").T @ xq
    out_0 = relu(f64(feat) + f64(feat) * g + h)
    return (out_0,) + planes(out_0)

@@ -1,0 +1,153 @@
+from contextlib import ExitStack
+
+import concourse.mybir as mybir
+
+K, T, S, N = 512, 2048, 512, 512
+FLOPS = 2 * 2 * K * N * S
+
+F32 = mybir.dt.float32
+BF16 = mybir.dt.bfloat16
+I32 = mybir.dt.int32
+U32 = mybir.dt.uint32
+U16 = mybir.dt.uint16
+U8 = mybir.dt.uint8
+FP8X4 = mybir.dt.float8_e4m3fn_x4
+ALU = mybir.AluOpType
+ACT = mybir.ActivationFunctionType
+
+P = 128
+PACK = 4
+CHUNK = 128
+CHUNKS = S // CHUNK
+M_VECTOR = (48, 84)
+
+
+def tile_picked_zfilm_relu_po_kernel(
+    tc, x_words, x_scales, w1, w2, feat, offs, out_0, out_1, out_2
+):
+    nc = tc.nc
+    with ExitStack() as ctx:
+        keep = ctx.enter_context(tc.tile_pool(name="keep", bufs=1))
+        psum = ctx.enter_context(tc.psum_pool(name="psum", bufs=1))
+
+        offsets = keep.tile([P, S // 16], U16, name="offsets")
+        table_words = keep.tile([P, T], U32, name="table_words", align_bytes=64)
+        table_scales = keep.tile([P, T], U8, name="table_scales", align_bytes=64)
+        w_raw = [keep.tile([P, PACK, N], F32, name=f"w_raw{i}", align_bytes=64) for i in range(2)]
+        feat_sb = [keep.tile([P, PACK, CHUNK], F32, name=f"feat{c}", align_bytes=64) for c in range(CHUNKS)]
+
+        nc.vector.memset(table_scales[:].bitcast(I32), 0)
+
+        nc.sync.dma_start(out=w_raw[0][:], in_=w1.rearrange("(p j) m -> p j m", j=PACK))
+        for q in range(4):
+            nc.sync.dma_start(
+                out=table_scales[32 * q : 32 * q + 4, :].bitcast(I32),
+                in_=x_scales[0][4 * q : 4 * q + 4, :].bitcast(I32),
+            )
+        nc.sync.dma_start(offsets[:], offs)
+        nc.sync.dma_start(out=w_raw[1][:], in_=w2.rearrange("(p j) m -> p j m", j=PACK))
+        nc.sync.dma_start(
+            out=table_words[:].bitcast(I32),
+            in_=x_words[0].rearrange("p c r -> p (c r)").bitcast(I32),
+        )
+        feat_rows = feat.rearrange("(p t) s -> p t s", t=PACK)
+        for c in range(CHUNKS):
+            nc.sync.dma_start(out=feat_sb[c][:], in_=feat_rows[:, :, c * CHUNK : (c + 1) * CHUNK])
+
+        w_bf = [keep.tile([P, PACK, P, PACK], BF16, name=f"w_bf{i}", align_bytes=64) for i in range(2)]
+        w_codes = [keep.tile([P, N], U32, name=f"w_codes{i}", align_bytes=64) for i in range(2)]
+        w_scales = [keep.tile([P, N], U8, name=f"w_scales{i}", align_bytes=64) for i in range(2)]
+
+        def quantize_weight(i):
+            src = w_raw[i][:].rearrange("p j (m t) -> p m t j", t=PACK)
+            dst = w_bf[i][:].rearrange("p t m j -> p m t j")
+            nc.vector.tensor_copy(out=dst[:, :M_VECTOR[i]], in_=src[:, :M_VECTOR[i]])
+            nc.scalar.activation(out=dst[:, M_VECTOR[i]:], in_=src[:, M_VECTOR[i]:], func=ACT.Copy)
+            nc.vector.quantize_mx(
+                out=w_codes[i][:].bitcast(FP8X4),
+                scales=w_scales[i][:],
+                in_=w_bf[i][:].rearrange("p t m j -> p (t m j)"),
+            )
+
+        words_first = keep.tile([P, CHUNK], U32, name="words_first", align_bytes=64)
+        words_rest = keep.tile([P, S - CHUNK], U32, name="words_rest", align_bytes=64)
+        picked_words = [words_first[:]] + [words_rest[:, c * CHUNK : (c + 1) * CHUNK] for c in range(CHUNKS - 1)]
+        picked_scales = keep.tile([P, S], U8, name="picked_scales", align_bytes=64)
+
+        def product(i, c):
+            bank = psum.tile([P, PACK, CHUNK], F32, name=f"bank{i}_{c}")
+            cols = slice(c * CHUNK, (c + 1) * CHUNK)
+            for t in range(PACK):
+                rows = slice(t * P, (t + 1) * P)
+                nc.tensor.matmul_mx(
+                    out=bank[:, t, :],
+                    lhsT=w_codes[i][:, rows].bitcast(FP8X4),
+                    lhsT_scale=w_scales[i][:, rows],
+                    rhs=picked_words[c].bitcast(FP8X4),
+                    rhs_scale=picked_scales[:, cols],
+                    start=True,
+                    stop=True,
+                )
+            return bank
+
+        quantize_weight(0)
+        nc.vector.tensor_copy(picked_scales[:], table_scales[:].indirect(offsets[:]))
+        quantize_weight(1)
+        nc.vector.tensor_copy(words_first[:], table_words[:].indirect(offsets[:, : CHUNK // 16]))
+        nc.vector.tensor_copy(words_rest[:], table_words[:].indirect(offsets[:, CHUNK // 16 :]))
+        g, h = [product(0, 0)], []
+        for c in range(CHUNKS):
+            if c + 1 < CHUNKS:
+                g.append(product(0, c + 1))
+            h.append(product(1, c))
+
+        y_codes = keep.tile([P, S], U32, name="y_codes", align_bytes=64)
+        y_scales = keep.tile([P, S], U8, name="y_scales", align_bytes=64)
+        scaled = [keep.tile([P, PACK, CHUNK], F32, name=f"scaled{c}", align_bytes=64) for c in range(CHUNKS)]
+        summed = [keep.tile([P, PACK, CHUNK], F32, name=f"summed{c}", align_bytes=64) for c in range(CHUNKS)]
+        y = [keep.tile([P, PACK, CHUNK], F32, name=f"y{c}", align_bytes=64) for c in range(CHUNKS)]
+        y_bf = [keep.tile([P, CHUNK, PACK], BF16, name=f"y_bf{c}", align_bytes=64) for c in range(CHUNKS)]
+        out_rows = out_0.rearrange("(p t) s -> p t s", t=PACK)
+        out_words = out_1[0].rearrange("p c r -> p (c r)").bitcast(I32)
+
+        def scale_step(c):
+            nc.vector.scalar_tensor_tensor(
+                out=scaled[c][:], in0=g[c][:], scalar=1.0, in1=feat_sb[c][:], op0=ALU.add, op1=ALU.mult
+            )
+
+        def shift_step(c):
+            nc.vector.tensor_tensor(out=summed[c][:], in0=h[c][:], in1=scaled[c][:], op=ALU.add)
+            nc.scalar.activation(out=y[c][:], in_=summed[c][:], func=ACT.Relu)
+            queue = nc.sync if c < CHUNKS - 1 else nc.scalar
+            queue.dma_start(out=out_rows[:, :, c * CHUNK : (c + 1) * CHUNK], in_=y[c][:])
+            by_column = summed[c][:].rearrange("p t s -> p s t")
+            if c < CHUNKS - 1:
+                nc.scalar.activation(out=y_bf[c][:], in_=by_column, func=ACT.Relu)
+            else:
+                nc.vector.tensor_scalar_max(out=y_bf[c][:], in0=by_column, scalar1=0.0)
+
+        def quantize_step(c):
+            cols = slice(c * CHUNK, (c + 1) * CHUNK)
+            nc.vector.quantize_mx(
+                out=y_codes[:, cols].bitcast(FP8X4),
+                scales=y_scales[:, cols],
+                in_=y_bf[c][:].rearrange("p s t -> p (s t)"),
+            )
+
+        scale_step(0)
+        for c in range(CHUNKS):
+            if c + 1 < CHUNKS:
+                scale_step(c + 1)
+            shift_step(c)
+            if c > 0:
+                quantize_step(c - 1)
+        split = (CHUNKS - 1) * CHUNK
+        nc.sync.dma_start(out=out_words[:, :split], in_=y_codes[:, :split].bitcast(I32))
+        quantize_step(CHUNKS - 1)
+        nc.sync.dma_start(out=out_words[:, split:], in_=y_codes[:, split:].bitcast(I32))
+        for q in range(4):
+            queue = nc.scalar if q % 2 else nc.sync
+            queue.dma_start(
+                out=out_2[0][4 * q : 4 * q + 4, :].bitcast(I32),
+                in_=y_scales[32 * q : 32 * q + 4, :].bitcast(I32),
+            )

@@ -19,7 +19,7 @@ P = 128
 PACK = 4
 CHUNK = 128
 CHUNKS = S // CHUNK
-M_VECTOR = (48, 84)
+M_VECTOR = (48, 80)
 
 
 def tile_picked_zfilm_relu_po_kernel(
@@ -34,25 +34,26 @@ def tile_picked_zfilm_relu_po_kernel(
         table_words = keep.tile([P, T], U32, name="table_words", align_bytes=64)
         table_scales = keep.tile([P, T], U8, name="table_scales", align_bytes=64)
         w_raw = [keep.tile([P, PACK, N], F32, name=f"w_raw{i}", align_bytes=64) for i in range(2)]
-        feat_sb = [keep.tile([P, PACK, CHUNK], F32, name=f"feat{c}", align_bytes=64) for c in range(CHUNKS)]
+        feat_pairs = [keep.tile([P, PACK, 2 * CHUNK], F32, name=f"feat{i}", align_bytes=64) for i in range(2)]
+        feat_sb = [feat_pairs[c // 2][:, :, (c % 2) * CHUNK : (c % 2 + 1) * CHUNK] for c in range(CHUNKS)]
 
         nc.vector.memset(table_scales[:].bitcast(I32), 0)
 
         nc.sync.dma_start(out=w_raw[0][:], in_=w1.rearrange("(p j) m -> p j m", j=PACK))
-        for q in range(4):
+        for r in range(4):
             nc.sync.dma_start(
-                out=table_scales[32 * q : 32 * q + 4, :].bitcast(I32),
-                in_=x_scales[0][4 * q : 4 * q + 4, :].bitcast(I32),
+                out=table_scales[r:P:32, :].bitcast(I32),
+                in_=x_scales[0][r:16:4, :].bitcast(I32),
             )
         nc.sync.dma_start(offsets[:], offs)
-        nc.sync.dma_start(out=w_raw[1][:], in_=w2.rearrange("(p j) m -> p j m", j=PACK))
         nc.sync.dma_start(
             out=table_words[:].bitcast(I32),
             in_=x_words[0].rearrange("p c r -> p (c r)").bitcast(I32),
         )
+        nc.sync.dma_start(out=w_raw[1][:], in_=w2.rearrange("(p j) m -> p j m", j=PACK))
         feat_rows = feat.rearrange("(p t) s -> p t s", t=PACK)
-        for c in range(CHUNKS):
-            nc.sync.dma_start(out=feat_sb[c][:], in_=feat_rows[:, :, c * CHUNK : (c + 1) * CHUNK])
+        for i in range(2):
+            nc.sync.dma_start(out=feat_pairs[i][:], in_=feat_rows[:, :, 2 * i * CHUNK : 2 * (i + 1) * CHUNK])
 
         w_bf = [keep.tile([P, PACK, P, PACK], BF16, name=f"w_bf{i}", align_bytes=64) for i in range(2)]
         w_codes = [keep.tile([P, N], U32, name=f"w_codes{i}", align_bytes=64) for i in range(2)]
@@ -69,9 +70,7 @@ def tile_picked_zfilm_relu_po_kernel(
                 in_=w_bf[i][:].rearrange("p t m j -> p (t m j)"),
             )
 
-        words_first = keep.tile([P, CHUNK], U32, name="words_first", align_bytes=64)
-        words_rest = keep.tile([P, S - CHUNK], U32, name="words_rest", align_bytes=64)
-        picked_words = [words_first[:]] + [words_rest[:, c * CHUNK : (c + 1) * CHUNK] for c in range(CHUNKS - 1)]
+        picked_words = keep.tile([P, S], U32, name="picked_words", align_bytes=64)
         picked_scales = keep.tile([P, S], U8, name="picked_scales", align_bytes=64)
 
         def product(i, c):
@@ -83,7 +82,7 @@ def tile_picked_zfilm_relu_po_kernel(
                     out=bank[:, t, :],
                     lhsT=w_codes[i][:, rows].bitcast(FP8X4),
                     lhsT_scale=w_scales[i][:, rows],
-                    rhs=picked_words[c].bitcast(FP8X4),
+                    rhs=picked_words[:, cols].bitcast(FP8X4),
                     rhs_scale=picked_scales[:, cols],
                     start=True,
                     stop=True,
@@ -92,14 +91,10 @@ def tile_picked_zfilm_relu_po_kernel(
 
         quantize_weight(0)
         nc.vector.tensor_copy(picked_scales[:], table_scales[:].indirect(offsets[:]))
+        nc.vector.tensor_copy(picked_words[:], table_words[:].indirect(offsets[:]))
+        g = [product(0, c) for c in range(CHUNKS)]
         quantize_weight(1)
-        nc.vector.tensor_copy(words_first[:], table_words[:].indirect(offsets[:, : CHUNK // 16]))
-        nc.vector.tensor_copy(words_rest[:], table_words[:].indirect(offsets[:, CHUNK // 16 :]))
-        g, h = [product(0, 0)], []
-        for c in range(CHUNKS):
-            if c + 1 < CHUNKS:
-                g.append(product(0, c + 1))
-            h.append(product(1, c))
+        h = [product(1, c) for c in range(CHUNKS)]
 
         y_codes = keep.tile([P, S], U32, name="y_codes", align_bytes=64)
         y_scales = keep.tile([P, S], U8, name="y_scales", align_bytes=64)
@@ -112,7 +107,7 @@ def tile_picked_zfilm_relu_po_kernel(
 
         def scale_step(c):
             nc.vector.scalar_tensor_tensor(
-                out=scaled[c][:], in0=g[c][:], scalar=1.0, in1=feat_sb[c][:], op0=ALU.add, op1=ALU.mult
+                out=scaled[c][:], in0=g[c][:], scalar=1.0, in1=feat_sb[c], op0=ALU.add, op1=ALU.mult
             )
 
         def shift_step(c):
@@ -120,8 +115,10 @@ def tile_picked_zfilm_relu_po_kernel(
             nc.scalar.activation(out=y[c][:], in_=summed[c][:], func=ACT.Relu)
             queue = nc.sync if c < CHUNKS - 1 else nc.scalar
             queue.dma_start(out=out_rows[:, :, c * CHUNK : (c + 1) * CHUNK], in_=y[c][:])
+
+        def round_step(c):
             by_column = summed[c][:].rearrange("p t s -> p s t")
-            if c < CHUNKS - 1:
+            if c < CHUNKS // 2:
                 nc.scalar.activation(out=y_bf[c][:], in_=by_column, func=ACT.Relu)
             else:
                 nc.vector.tensor_scalar_max(out=y_bf[c][:], in0=by_column, scalar1=0.0)
@@ -135,19 +132,27 @@ def tile_picked_zfilm_relu_po_kernel(
             )
 
         scale_step(0)
-        for c in range(CHUNKS):
-            if c + 1 < CHUNKS:
-                scale_step(c + 1)
-            shift_step(c)
-            if c > 0:
-                quantize_step(c - 1)
-        split = (CHUNKS - 1) * CHUNK
-        nc.sync.dma_start(out=out_words[:, :split], in_=y_codes[:, :split].bitcast(I32))
-        quantize_step(CHUNKS - 1)
-        nc.sync.dma_start(out=out_words[:, split:], in_=y_codes[:, split:].bitcast(I32))
-        for q in range(4):
-            queue = nc.scalar if q % 2 else nc.sync
+        scale_step(1)
+        shift_step(0)
+        round_step(0)
+        scale_step(2)
+        shift_step(1)
+        round_step(1)
+        scale_step(3)
+        quantize_step(0)
+        shift_step(2)
+        shift_step(3)
+        quantize_step(1)
+        half = S // 2
+        nc.sync.dma_start(out=out_words[:, :half], in_=y_codes[:, :half].bitcast(I32))
+        round_step(2)
+        round_step(3)
+        quantize_step(2)
+        quantize_step(3)
+        nc.sync.dma_start(out=out_words[:, half:], in_=y_codes[:, half:].bitcast(I32))
+        for r in range(4):
+            queue = nc.scalar if r % 2 == 0 else nc.sync
             queue.dma_start(
-                out=out_2[0][4 * q : 4 * q + 4, :].bitcast(I32),
-                in_=y_scales[32 * q : 32 * q + 4, :].bitcast(I32),
+                out=out_2[0][r:16:4, :].bitcast(I32),
+                in_=y_scales[r:P:32, :].bitcast(I32),
             )

@@ -17,9 +17,15 @@ ACT = mybir.ActivationFunctionType
 
 P = 128
 PACK = 4
-CHUNK = 128
-CHUNKS = S // CHUNK
+HALF = S // 2
+UNITS = 4
+STRIP = 128
 M_VECTOR = (48, 80)
+
+
+def unit_of(rows, u):
+    half, pair = divmod(u, 2)
+    return rows[:, 2 * pair : 2 * pair + 2, half * HALF : (half + 1) * HALF]
 
 
 def tile_picked_zfilm_relu_po_kernel(
@@ -34,8 +40,7 @@ def tile_picked_zfilm_relu_po_kernel(
         table_words = keep.tile([P, T], U32, name="table_words", align_bytes=64)
         table_scales = keep.tile([P, T], U8, name="table_scales", align_bytes=64)
         w_raw = [keep.tile([P, PACK, N], F32, name=f"w_raw{i}", align_bytes=64) for i in range(2)]
-        feat_pairs = [keep.tile([P, PACK, 2 * CHUNK], F32, name=f"feat{i}", align_bytes=64) for i in range(2)]
-        feat_sb = [feat_pairs[c // 2][:, :, (c % 2) * CHUNK : (c % 2 + 1) * CHUNK] for c in range(CHUNKS)]
+        feat_sb = [keep.tile([P, 2, HALF], F32, name=f"feat{u}", align_bytes=64) for u in range(UNITS)]
 
         nc.vector.memset(table_scales[:].bitcast(I32), 0)
 
@@ -52,8 +57,8 @@ def tile_picked_zfilm_relu_po_kernel(
         )
         nc.sync.dma_start(out=w_raw[1][:], in_=w2.rearrange("(p j) m -> p j m", j=PACK))
         feat_rows = feat.rearrange("(p t) s -> p t s", t=PACK)
-        for i in range(2):
-            nc.sync.dma_start(out=feat_pairs[i][:], in_=feat_rows[:, :, 2 * i * CHUNK : 2 * (i + 1) * CHUNK])
+        for u in range(UNITS):
+            nc.sync.dma_start(out=feat_sb[u][:], in_=unit_of(feat_rows, u))
 
         w_bf = [keep.tile([P, PACK, P, PACK], BF16, name=f"w_bf{i}", align_bytes=64) for i in range(2)]
         w_codes = [keep.tile([P, N], U32, name=f"w_codes{i}", align_bytes=64) for i in range(2)]
@@ -64,22 +69,25 @@ def tile_picked_zfilm_relu_po_kernel(
             dst = w_bf[i][:].rearrange("p t m j -> p m t j")
             nc.vector.tensor_copy(out=dst[:, :M_VECTOR[i]], in_=src[:, :M_VECTOR[i]])
             nc.scalar.activation(out=dst[:, M_VECTOR[i]:], in_=src[:, M_VECTOR[i]:], func=ACT.Copy)
-            nc.vector.quantize_mx(
-                out=w_codes[i][:].bitcast(FP8X4),
-                scales=w_scales[i][:],
-                in_=w_bf[i][:].rearrange("p t m j -> p (t m j)"),
-            )
+            for pair in range(2):
+                cols = slice(pair * 2 * P, (pair + 1) * 2 * P)
+                nc.vector.quantize_mx(
+                    out=w_codes[i][:, cols].bitcast(FP8X4),
+                    scales=w_scales[i][:, cols],
+                    in_=w_bf[i][:, 2 * pair : 2 * pair + 2].rearrange("p t m j -> p (t m j)"),
+                )
 
         picked_words = keep.tile([P, S], U32, name="picked_words", align_bytes=64)
         picked_scales = keep.tile([P, S], U8, name="picked_scales", align_bytes=64)
 
-        def product(i, c):
-            bank = psum.tile([P, PACK, CHUNK], F32, name=f"bank{i}_{c}")
-            cols = slice(c * CHUNK, (c + 1) * CHUNK)
-            for t in range(PACK):
-                rows = slice(t * P, (t + 1) * P)
+        def product(i, u):
+            half, pair = divmod(u, 2)
+            bank = psum.tile([P, 2, HALF], F32, name=f"bank{i}_{u}")
+            cols = slice(half * HALF, (half + 1) * HALF)
+            for e in range(2):
+                rows = slice((2 * pair + e) * P, (2 * pair + e + 1) * P)
                 nc.tensor.matmul_mx(
-                    out=bank[:, t, :],
+                    out=bank[:, e, :],
                     lhsT=w_codes[i][:, rows].bitcast(FP8X4),
                     lhsT_scale=w_scales[i][:, rows],
                     rhs=picked_words[:, cols].bitcast(FP8X4),
@@ -92,64 +100,71 @@ def tile_picked_zfilm_relu_po_kernel(
         quantize_weight(0)
         nc.vector.tensor_copy(picked_scales[:], table_scales[:].indirect(offsets[:]))
         nc.vector.tensor_copy(picked_words[:], table_words[:].indirect(offsets[:]))
-        g = [product(0, c) for c in range(CHUNKS)]
+        g = [product(0, u) for u in range(UNITS)]
         quantize_weight(1)
-        h = [product(1, c) for c in range(CHUNKS)]
+        h = [product(1, u) for u in range(UNITS)]
 
         y_codes = keep.tile([P, S], U32, name="y_codes", align_bytes=64)
         y_scales = keep.tile([P, S], U8, name="y_scales", align_bytes=64)
-        scaled = [keep.tile([P, PACK, CHUNK], F32, name=f"scaled{c}", align_bytes=64) for c in range(CHUNKS)]
-        summed = [keep.tile([P, PACK, CHUNK], F32, name=f"summed{c}", align_bytes=64) for c in range(CHUNKS)]
-        y = [keep.tile([P, PACK, CHUNK], F32, name=f"y{c}", align_bytes=64) for c in range(CHUNKS)]
-        y_bf = [keep.tile([P, CHUNK, PACK], BF16, name=f"y_bf{c}", align_bytes=64) for c in range(CHUNKS)]
+        scaled = [keep.tile([P, 2, HALF], F32, name=f"scaled{u}", align_bytes=64) for u in range(UNITS)]
+        summed = [keep.tile([P, PACK, HALF], F32, name=f"summed{i}", align_bytes=64) for i in range(2)]
+        y = [keep.tile([P, 2, HALF], F32, name=f"y{u}", align_bytes=64) for u in range(UNITS)]
+        y_bf = [keep.tile([P, STRIP, PACK], BF16, name=f"y_bf{c}", align_bytes=64) for c in range(S // STRIP)]
         out_rows = out_0.rearrange("(p t) s -> p t s", t=PACK)
         out_words = out_1[0].rearrange("p c r -> p (c r)").bitcast(I32)
 
-        def scale_step(c):
+        def scale_step(u):
             nc.vector.scalar_tensor_tensor(
-                out=scaled[c][:], in0=g[c][:], scalar=1.0, in1=feat_sb[c], op0=ALU.add, op1=ALU.mult
+                out=scaled[u][:], in0=g[u][:], scalar=1.0, in1=feat_sb[u][:], op0=ALU.add, op1=ALU.mult
             )
 
-        def shift_step(c):
-            nc.vector.tensor_tensor(out=summed[c][:], in0=h[c][:], in1=scaled[c][:], op=ALU.add)
-            nc.scalar.activation(out=y[c][:], in_=summed[c][:], func=ACT.Relu)
-            queue = nc.sync if c < CHUNKS - 1 else nc.scalar
-            queue.dma_start(out=out_rows[:, :, c * CHUNK : (c + 1) * CHUNK], in_=y[c][:])
+        def scale_step_gpsimd(u):
+            gain = w_raw[1][:, u, :].rearrange("p (e s) -> p e s", e=2)
+            nc.scalar.activation(out=gain, in_=g[u][:], func=ACT.Copy, bias=1.0)
+            nc.gpsimd.tensor_tensor(out=scaled[u][:], in0=gain, in1=feat_sb[u][:], op=ALU.mult)
+
+        def shift_step(u):
+            half, pair = divmod(u, 2)
+            total = summed[half][:, 2 * pair : 2 * pair + 2, :]
+            nc.vector.tensor_tensor(out=total, in0=h[u][:], in1=scaled[u][:], op=ALU.add)
+            nc.scalar.activation(out=y[u][:], in_=total, func=ACT.Relu)
+            queue = nc.sync if u < UNITS - 1 else nc.scalar
+            queue.dma_start(out=unit_of(out_rows, u), in_=y[u][:])
 
         def round_step(c):
-            by_column = summed[c][:].rearrange("p t s -> p s t")
-            if c < CHUNKS // 2:
+            half, part = divmod(c, 2)
+            by_column = summed[half][:, :, part * STRIP : (part + 1) * STRIP].rearrange("p t s -> p s t")
+            if c < 1:
                 nc.scalar.activation(out=y_bf[c][:], in_=by_column, func=ACT.Relu)
             else:
                 nc.vector.tensor_scalar_max(out=y_bf[c][:], in0=by_column, scalar1=0.0)
 
         def quantize_step(c):
-            cols = slice(c * CHUNK, (c + 1) * CHUNK)
+            cols = slice(c * STRIP, (c + 1) * STRIP)
             nc.vector.quantize_mx(
                 out=y_codes[:, cols].bitcast(FP8X4),
                 scales=y_scales[:, cols],
                 in_=y_bf[c][:].rearrange("p s t -> p (s t)"),
             )
 
+        scale_step_gpsimd(1)
+        scale_step_gpsimd(3)
         scale_step(0)
-        scale_step(1)
-        shift_step(0)
-        round_step(0)
         scale_step(2)
+        shift_step(0)
         shift_step(1)
-        round_step(1)
-        scale_step(3)
-        quantize_step(0)
+        round_step(0)
         shift_step(2)
         shift_step(3)
-        quantize_step(1)
-        half = S // 2
-        nc.sync.dma_start(out=out_words[:, :half], in_=y_codes[:, :half].bitcast(I32))
+        round_step(1)
+        quantize_step(0)
         round_step(2)
+        quantize_step(1)
+        nc.sync.dma_start(out=out_words[:, :HALF], in_=y_codes[:, :HALF].bitcast(I32))
         round_step(3)
         quantize_step(2)
         quantize_step(3)
-        nc.sync.dma_start(out=out_words[:, half:], in_=y_codes[:, half:].bitcast(I32))
+        nc.sync.dma_start(out=out_words[:, HALF:], in_=y_codes[:, HALF:].bitcast(I32))
         for r in range(4):
             queue = nc.scalar if r % 2 == 0 else nc.sync
             queue.dma_start(

@@ -20,6 +20,8 @@ PACK = 4
 HALF = S // 2
 UNITS = 4
 STRIP = 128
+GPSIMD_COLS = 192
+NEED_ORDER = (0, 2, 1, 3)
 M_VECTOR = (48, 80)
 
 
@@ -57,7 +59,7 @@ def tile_picked_zfilm_relu_po_kernel(
         )
         nc.sync.dma_start(out=w_raw[1][:], in_=w2.rearrange("(p j) m -> p j m", j=PACK))
         feat_rows = feat.rearrange("(p t) s -> p t s", t=PACK)
-        for u in range(UNITS):
+        for u in NEED_ORDER:
             nc.sync.dma_start(out=feat_sb[u][:], in_=unit_of(feat_rows, u))
 
         w_bf = [keep.tile([P, PACK, P, PACK], BF16, name=f"w_bf{i}", align_bytes=64) for i in range(2)]
@@ -100,7 +102,7 @@ def tile_picked_zfilm_relu_po_kernel(
         quantize_weight(0)
         nc.vector.tensor_copy(picked_scales[:], table_scales[:].indirect(offsets[:]))
         nc.vector.tensor_copy(picked_words[:], table_words[:].indirect(offsets[:]))
-        g = [product(0, u) for u in range(UNITS)]
+        g = {u: product(0, u) for u in NEED_ORDER}
         quantize_weight(1)
         h = [product(1, u) for u in range(UNITS)]
 
@@ -108,33 +110,44 @@ def tile_picked_zfilm_relu_po_kernel(
         y_scales = keep.tile([P, S], U8, name="y_scales", align_bytes=64)
         scaled = [keep.tile([P, 2, HALF], F32, name=f"scaled{u}", align_bytes=64) for u in range(UNITS)]
         summed = [keep.tile([P, PACK, HALF], F32, name=f"summed{i}", align_bytes=64) for i in range(2)]
-        y = [keep.tile([P, 2, HALF], F32, name=f"y{u}", align_bytes=64) for u in range(UNITS)]
+        y = [keep.tile([P, PACK, HALF], F32, name=f"y{i}", align_bytes=64) for i in range(2)]
         y_bf = [keep.tile([P, STRIP, PACK], BF16, name=f"y_bf{c}", align_bytes=64) for c in range(S // STRIP)]
         out_rows = out_0.rearrange("(p t) s -> p t s", t=PACK)
         out_words = out_1[0].rearrange("p c r -> p (c r)").bitcast(I32)
 
-        def scale_step(u):
+        def scale_step(u, cols=slice(0, HALF)):
             nc.vector.scalar_tensor_tensor(
-                out=scaled[u][:], in0=g[u][:], scalar=1.0, in1=feat_sb[u][:], op0=ALU.add, op1=ALU.mult
+                out=scaled[u][:, :, cols],
+                in0=g[u][:, :, cols],
+                scalar=1.0,
+                in1=feat_sb[u][:, :, cols],
+                op0=ALU.add,
+                op1=ALU.mult,
             )
 
-        def scale_step_gpsimd(u):
-            gain = w_raw[1][:, u, :].rearrange("p (e s) -> p e s", e=2)
-            nc.scalar.activation(out=gain, in_=g[u][:], func=ACT.Copy, bias=1.0)
-            nc.gpsimd.tensor_tensor(out=scaled[u][:], in0=gain, in1=feat_sb[u][:], op=ALU.mult)
+        def scale_step_gpsimd(u, cols=slice(0, HALF)):
+            gain = w_raw[1][:, u, :].rearrange("p (e s) -> p e s", e=2)[:, :, cols]
+            nc.scalar.activation(out=gain, in_=g[u][:, :, cols], func=ACT.Copy, bias=1.0)
+            nc.gpsimd.tensor_tensor(out=scaled[u][:, :, cols], in0=gain, in1=feat_sb[u][:, :, cols], op=ALU.mult)
 
         def shift_step(u):
             half, pair = divmod(u, 2)
             total = summed[half][:, 2 * pair : 2 * pair + 2, :]
             nc.vector.tensor_tensor(out=total, in0=h[u][:], in1=scaled[u][:], op=ALU.add)
-            nc.scalar.activation(out=y[u][:], in_=total, func=ACT.Relu)
+            y_unit = y[half][:, 2 * pair : 2 * pair + 2, :]
+            nc.scalar.activation(out=y_unit, in_=total, func=ACT.Relu)
             queue = nc.sync if u < UNITS - 1 else nc.scalar
-            queue.dma_start(out=unit_of(out_rows, u), in_=y[u][:])
+            queue.dma_start(out=unit_of(out_rows, u), in_=y_unit)
 
         def round_step(c):
             half, part = divmod(c, 2)
             by_column = summed[half][:, :, part * STRIP : (part + 1) * STRIP].rearrange("p t s -> p s t")
-            if c < 1:
+            if c == 0:
+                y_by_column = y[half][:, :, part * STRIP : (part + 1) * STRIP].rearrange("p t s -> p s t")
+                nc.gpsimd.tensor_scalar(
+                    out=y_bf[c][:], in0=y_by_column, scalar1=1.0, scalar2=0.0, op0=ALU.mult, op1=ALU.add
+                )
+            elif c == 1:
                 nc.scalar.activation(out=y_bf[c][:], in_=by_column, func=ACT.Relu)
             else:
                 nc.vector.tensor_scalar_max(out=y_bf[c][:], in0=by_column, scalar1=0.0)
@@ -147,19 +160,20 @@ def tile_picked_zfilm_relu_po_kernel(
                 in_=y_bf[c][:].rearrange("p s t -> p (s t)"),
             )
 
-        scale_step_gpsimd(1)
-        scale_step_gpsimd(3)
+        scale_step_gpsimd(2)
+        scale_step_gpsimd(3, slice(0, GPSIMD_COLS))
         scale_step(0)
-        scale_step(2)
+        scale_step(1)
         shift_step(0)
         shift_step(1)
+        round_step(1)
         round_step(0)
+        scale_step(3, slice(GPSIMD_COLS, HALF))
         shift_step(2)
         shift_step(3)
-        round_step(1)
-        quantize_step(0)
-        round_step(2)
         quantize_step(1)
+        round_step(2)
+        quantize_step(0)
         nc.sync.dma_start(out=out_words[:, :HALF], in_=y_codes[:, :HALF].bitcast(I32))
         round_step(3)
         quantize_step(2)

from contextlib import ExitStack

import concourse.mybir as mybir

K, T, S, N = 512, 2048, 512, 512
FLOPS = 2 * 2 * K * N * S

F32 = mybir.dt.float32
BF16 = mybir.dt.bfloat16
I32 = mybir.dt.int32
U32 = mybir.dt.uint32
U16 = mybir.dt.uint16
U8 = mybir.dt.uint8
FP8X4 = mybir.dt.float8_e4m3fn_x4
ALU = mybir.AluOpType
ACT = mybir.ActivationFunctionType

P = 128
PACK = 4
HALF = S // 2
UNITS = 4
STRIP = 128
GPSIMD_COLS = 192
NEED_ORDER = (0, 2, 1, 3)
M_VECTOR = (48, 80)


def unit_of(rows, u):
    half, pair = divmod(u, 2)
    return rows[:, 2 * pair : 2 * pair + 2, half * HALF : (half + 1) * HALF]


def tile_picked_zfilm_relu_po_kernel(
    tc, x_words, x_scales, w1, w2, feat, offs, out_0, out_1, out_2
):
    nc = tc.nc
    with ExitStack() as ctx:
        keep = ctx.enter_context(tc.tile_pool(name="keep", bufs=1))
        psum = ctx.enter_context(tc.psum_pool(name="psum", bufs=1))

        offsets = keep.tile([P, S // 16], U16, name="offsets")
        table_words = keep.tile([P, T], U32, name="table_words", align_bytes=64)
        table_scales = keep.tile([P, T], U8, name="table_scales", align_bytes=64)
        w_raw = [keep.tile([P, PACK, N], F32, name=f"w_raw{i}", align_bytes=64) for i in range(2)]
        feat_sb = [keep.tile([P, 2, HALF], F32, name=f"feat{u}", align_bytes=64) for u in range(UNITS)]

        nc.vector.memset(table_scales[:].bitcast(I32), 0)

        nc.sync.dma_start(out=w_raw[0][:], in_=w1.rearrange("(p j) m -> p j m", j=PACK))
        for r in range(4):
            nc.sync.dma_start(
                out=table_scales[r:P:32, :].bitcast(I32),
                in_=x_scales[0][r:16:4, :].bitcast(I32),
            )
        nc.sync.dma_start(offsets[:], offs)
        nc.sync.dma_start(
            out=table_words[:].bitcast(I32),
            in_=x_words[0].rearrange("p c r -> p (c r)").bitcast(I32),
        )
        nc.sync.dma_start(out=w_raw[1][:], in_=w2.rearrange("(p j) m -> p j m", j=PACK))
        feat_rows = feat.rearrange("(p t) s -> p t s", t=PACK)
        for u in NEED_ORDER:
            nc.sync.dma_start(out=feat_sb[u][:], in_=unit_of(feat_rows, u))

        w_bf = [keep.tile([P, PACK, P, PACK], BF16, name=f"w_bf{i}", align_bytes=64) for i in range(2)]
        w_codes = [keep.tile([P, N], U32, name=f"w_codes{i}", align_bytes=64) for i in range(2)]
        w_scales = [keep.tile([P, N], U8, name=f"w_scales{i}", align_bytes=64) for i in range(2)]

        def quantize_weight(i):
            src = w_raw[i][:].rearrange("p j (m t) -> p m t j", t=PACK)
            dst = w_bf[i][:].rearrange("p t m j -> p m t j")
            nc.vector.tensor_copy(out=dst[:, :M_VECTOR[i]], in_=src[:, :M_VECTOR[i]])
            nc.scalar.activation(out=dst[:, M_VECTOR[i]:], in_=src[:, M_VECTOR[i]:], func=ACT.Copy)
            for pair in range(2):
                cols = slice(pair * 2 * P, (pair + 1) * 2 * P)
                nc.vector.quantize_mx(
                    out=w_codes[i][:, cols].bitcast(FP8X4),
                    scales=w_scales[i][:, cols],
                    in_=w_bf[i][:, 2 * pair : 2 * pair + 2].rearrange("p t m j -> p (t m j)"),
                )

        picked_words = keep.tile([P, S], U32, name="picked_words", align_bytes=64)
        picked_scales = keep.tile([P, S], U8, name="picked_scales", align_bytes=64)

        def product(i, u):
            half, pair = divmod(u, 2)
            bank = psum.tile([P, 2, HALF], F32, name=f"bank{i}_{u}")
            cols = slice(half * HALF, (half + 1) * HALF)
            for e in range(2):
                rows = slice((2 * pair + e) * P, (2 * pair + e + 1) * P)
                nc.tensor.matmul_mx(
                    out=bank[:, e, :],
                    lhsT=w_codes[i][:, rows].bitcast(FP8X4),
                    lhsT_scale=w_scales[i][:, rows],
                    rhs=picked_words[:, cols].bitcast(FP8X4),
                    rhs_scale=picked_scales[:, cols],
                    start=True,
                    stop=True,
                )
            return bank

        quantize_weight(0)
        nc.vector.tensor_copy(picked_scales[:], table_scales[:].indirect(offsets[:]))
        nc.vector.tensor_copy(picked_words[:], table_words[:].indirect(offsets[:]))
        g = {u: product(0, u) for u in NEED_ORDER}
        quantize_weight(1)
        h = [product(1, u) for u in range(UNITS)]

        y_codes = keep.tile([P, S], U32, name="y_codes", align_bytes=64)
        y_scales = keep.tile([P, S], U8, name="y_scales", align_bytes=64)
        scaled = [keep.tile([P, 2, HALF], F32, name=f"scaled{u}", align_bytes=64) for u in range(UNITS)]
        summed = [keep.tile([P, PACK, HALF], F32, name=f"summed{i}", align_bytes=64) for i in range(2)]
        y = [keep.tile([P, PACK, HALF], F32, name=f"y{i}", align_bytes=64) for i in range(2)]
        y_bf = [keep.tile([P, STRIP, PACK], BF16, name=f"y_bf{c}", align_bytes=64) for c in range(S // STRIP)]
        out_rows = out_0.rearrange("(p t) s -> p t s", t=PACK)
        out_words = out_1[0].rearrange("p c r -> p (c r)").bitcast(I32)

        def scale_step(u, cols=slice(0, HALF)):
            nc.vector.scalar_tensor_tensor(
                out=scaled[u][:, :, cols],
                in0=g[u][:, :, cols],
                scalar=1.0,
                in1=feat_sb[u][:, :, cols],
                op0=ALU.add,
                op1=ALU.mult,
            )

        def scale_step_gpsimd(u, cols=slice(0, HALF)):
            gain = w_raw[1][:, u, :].rearrange("p (e s) -> p e s", e=2)[:, :, cols]
            nc.scalar.activation(out=gain, in_=g[u][:, :, cols], func=ACT.Copy, bias=1.0)
            nc.gpsimd.tensor_tensor(out=scaled[u][:, :, cols], in0=gain, in1=feat_sb[u][:, :, cols], op=ALU.mult)

        def shift_step(u):
            half, pair = divmod(u, 2)
            total = summed[half][:, 2 * pair : 2 * pair + 2, :]
            nc.vector.tensor_tensor(out=total, in0=h[u][:], in1=scaled[u][:], op=ALU.add)
            y_unit = y[half][:, 2 * pair : 2 * pair + 2, :]
            nc.scalar.activation(out=y_unit, in_=total, func=ACT.Relu)
            queue = nc.sync if u < UNITS - 1 else nc.scalar
            queue.dma_start(out=unit_of(out_rows, u), in_=y_unit)

        def round_step(c):
            half, part = divmod(c, 2)
            by_column = summed[half][:, :, part * STRIP : (part + 1) * STRIP].rearrange("p t s -> p s t")
            if c == 0:
                y_by_column = y[half][:, :, part * STRIP : (part + 1) * STRIP].rearrange("p t s -> p s t")
                nc.gpsimd.tensor_scalar(
                    out=y_bf[c][:], in0=y_by_column, scalar1=1.0, scalar2=0.0, op0=ALU.mult, op1=ALU.add
                )
            elif c == 1:
                nc.scalar.activation(out=y_bf[c][:], in_=by_column, func=ACT.Relu)
            else:
                nc.vector.tensor_scalar_max(out=y_bf[c][:], in0=by_column, scalar1=0.0)

        def quantize_step(c):
            cols = slice(c * STRIP, (c + 1) * STRIP)
            nc.vector.quantize_mx(
                out=y_codes[:, cols].bitcast(FP8X4),
                scales=y_scales[:, cols],
                in_=y_bf[c][:].rearrange("p s t -> p (s t)"),
            )

        scale_step_gpsimd(2)
        scale_step_gpsimd(3, slice(0, GPSIMD_COLS))
        scale_step(0)
        scale_step(1)
        shift_step(0)
        shift_step(1)
        round_step(1)
        round_step(0)
        scale_step(3, slice(GPSIMD_COLS, HALF))
        shift_step(2)
        shift_step(3)
        quantize_step(1)
        round_step(2)
        quantize_step(0)
        nc.sync.dma_start(out=out_words[:, :HALF], in_=y_codes[:, :HALF].bitcast(I32))
        round_step(3)
        quantize_step(2)
        quantize_step(3)
        nc.sync.dma_start(out=out_words[:, HALF:], in_=y_codes[:, HALF:].bitcast(I32))
        for r in range(4):
            queue = nc.scalar if r % 2 == 0 else nc.sync
            queue.dma_start(
                out=out_2[0][r:16:4, :].bitcast(I32),
                in_=y_scales[r:P:32, :].bitcast(I32),
            )
